import numpy as np
import ml_dtypes


def mxq(x, axis, fmt="e4m3"):
    dtype, down = {"e4m3": (ml_dtypes.float8_e4m3fn, 7), "e5m2": (ml_dtypes.float8_e5m2, 14)}[fmt]
    v = np.moveaxis(np.asarray(x, np.float32).astype(ml_dtypes.bfloat16).astype(np.float64), axis, -1)
    blocks = v.reshape(v.shape[:-1] + (-1, 32))
    amax = np.abs(blocks).max(-1, keepdims=True)
    byte = np.maximum(np.where(amax > 0, np.frexp(amax)[1] - 1 + 127, 0) - down, 1)
    scale = np.exp2(byte - 127.0)
    codes = (blocks / scale).astype(np.float32).astype(dtype).astype(np.float64)
    return np.moveaxis((codes * scale).reshape(v.shape), -1, axis)


WIDE = False


def mx_kscale(k):
    if not WIDE:
        return np.ones(k)
    levels = np.array([10, -10, 5, -5, 0])
    if k % 512:
        return np.exp2(np.random.permutation(np.resize(levels, k // 32))).repeat(32)
    a = np.empty((k // 512, 16))
    for p in range(k // 512):
        a[p, :8] = np.random.permutation(np.resize(levels, 8))
        for g in range(8):
            far = levels[np.abs(levels - a[p, g]) >= 10]
            a[p, g + 8] = far[np.random.randint(len(far))]
    return np.exp2(a.ravel()).repeat(32)


def f64(x):
    return np.asarray(x).astype(np.float64)


def striped(idx):
    return np.tile(np.asarray(idx).reshape(-1, 16).T, (8, 1)).astype(np.uint16)


def unstriped(offs):
    return offs[:16].T.reshape(-1).astype(np.int64)


E2M1 = np.array([0.0, 0.5, 1.0, 1.5, 2.0, 3.0, 4.0, 6.0, -0.0, -0.5, -1.0, -1.5, -2.0, -3.0, -4.0, -6.0])


def pack_weight(w, fmt):
    k, n = w.shape
    w = f64(np.asarray(w, np.float32).astype(ml_dtypes.bfloat16)).reshape(k // 32, 32, n)
    amax = np.abs(w).max(1)
    if fmt == "e4m3":
        byte = np.frexp(amax)[1] - 1 + 127 - 7
    else:
        mant, ex = np.frexp(amax / 6.0)
        byte = np.where(mant > 0.5, ex, ex - 1) + 127
    byte = np.clip(np.where(amax > 0, byte, 1), 1, 254)
    scaled = (w * np.exp2(127.0 - byte)[:, None, :]).reshape(k, n).astype(np.float32)
    by_word = np.ascontiguousarray(scaled.reshape(k // 512, 128, 4, n).transpose(0, 1, 3, 2))
    if fmt == "e4m3":
        words = by_word.astype(ml_dtypes.float8_e4m3fn).view(np.uint8)
    else:
        c = by_word.astype(ml_dtypes.float4_e2m1fn).view(np.uint8) & 0xF
        words = (c[..., 0::2] | (c[..., 1::2] << 4)).reshape(k // 512, 128, 2 * n)
    return np.ascontiguousarray(words), np.ascontiguousarray(byte.astype(np.uint8).reshape(k // 512, 16, n))


def unpack_weight(words, scales, fmt):
    g, _, n = scales.shape
    words = np.ascontiguousarray(words).reshape(g, 128, n, -1)
    if fmt == "e4m3":
        vals = words.view(ml_dtypes.float8_e4m3fn).astype(np.float64)
    else:
        nib = np.empty((g, 128, n, 4), np.uint8)
        nib[..., 0::2] = words & 0xF
        nib[..., 1::2] = words >> 4
        vals = E2M1[nib]
    vals = vals * np.repeat(np.exp2(scales.astype(np.float64) - 127.0), 8, axis=1)[..., None]
    return vals.transpose(0, 1, 3, 2).reshape(g * 512, n)


K, Q, J, T, V, X, S, N, E = 512, 128, 256, 1024, 512, 1024, 512, 256, 512


def setup_inputs():
    n = np.random.standard_normal
    idx = np.random.permutation(T)[:J]
    idx2 = np.random.permutation(V)[:J]
    idx3 = np.random.permutation(X)[:J]
    idx4 = np.random.permutation(S)[:J]
    idx5 = np.random.permutation(E)[:J]
    fk = mx_kscale(K)
    wp = pack_weight(n((K, N)) * 1 / np.sqrt(K) / fk[:, None], "e2m1")
    return {
        "ca": (np.random.randint(-7, 8, (Q, T)).astype(np.float64)).astype(np.float32),
        "ga": (np.random.uniform(0.1, 0.4, (Q, 1)) * fk[::4, None]).astype(np.float32),
        "cb": (np.random.randint(-7, 8, (Q, V)).astype(np.float64)).astype(np.float32),
        "gb": (np.random.uniform(0.1, 0.4, (Q, 1)) * fk[::4, None]).astype(np.float32),
        "cc": (np.random.randint(-7, 8, (Q, X)).astype(np.float64)).astype(np.float32),
        "gc": (np.random.uniform(0.1, 0.4, (Q, 1)) * fk[::4, None]).astype(np.float32),
        "cd": (np.random.randint(-7, 8, (Q, S)).astype(np.float64)).astype(np.float32),
        "gd": (np.random.uniform(0.1, 0.4, (Q, 1)) * fk[::4, None]).astype(np.float32),
        "w_words": wp[0],
        "w_scales": wp[1],
        "so": (np.random.uniform(0.5, 1.6, (N, 1))).astype(np.float32),
        "offs": striped(idx),
        "offs2": striped(idx2),
        "offs3": striped(idx3),
        "offs4": striped(idx4),
        "offs5": striped(idx5),
    }


def reference(ca, ga, cb, gb, cc, gc, cd, gd, w_words, w_scales, so, offs, offs2, offs3, offs4, offs5):
    idx = unstriped(offs)
    idx2 = unstriped(offs2)
    idx3 = unstriped(offs3)
    idx4 = unstriped(offs4)
    idx5 = unstriped(offs5)
    wu = unpack_weight(w_words, w_scales, "e2m1")
    v0 = f64(ca)[:, idx] * f64(ga)
    v1 = f64(cb)[:, idx2] * f64(gb)
    v2 = f64(cc)[:, idx3] * f64(gc)
    v3 = f64(cd)[:, idx4] * f64(gd)
    z = np.stack([v0, v1, v2, v3], axis=1).reshape(K, J)
    zq = mxq(z, 0, "e4m3")
    p = wu.T @ zq
    y = np.zeros((N, E))
    y[:, idx5] = p * f64(so)
    return y

@@ -1,0 +1,114 @@
+from contextlib import ExitStack
+
+import concourse.mybir as mybir
+
+K, J, N, E = 512, 256, 256, 512
+FLOPS = 2 * K * N * J
+
+F32 = mybir.dt.float32
+BF16 = mybir.dt.bfloat16
+I32 = mybir.dt.int32
+U32 = mybir.dt.uint32
+U16 = mybir.dt.uint16
+U8 = mybir.dt.uint8
+FP8X4 = mybir.dt.float8_e4m3fn_x4
+FP4X4 = mybir.dt.float4_e2m1fn_x4
+COPY = mybir.ActivationFunctionType.Copy
+
+P = 128
+PACK = 4
+HALF = J // 2
+LIST_COLS = J // 16
+
+
+def tile_list_fourtables_kernel(tc, ca, ga, cb, gb, cc, gc, cd, gd, w_words, w_scales, so, offs, offs2, offs3, offs4, offs5, out):
+    nc = tc.nc
+    with ExitStack() as ctx:
+        sb = ctx.enter_context(tc.tile_pool(name="sb", bufs=1))
+        psum = ctx.enter_context(tc.psum_pool(name="psum", bufs=1))
+
+        tables = [sb.tile(list(src.shape), F32, name="table%d" % t) for t, src in enumerate((ca, cb, cc, cd))]
+        steps = [sb.tile([P, 1], F32, name="step%d" % t) for t in range(PACK)]
+        lists = [sb.tile([P, LIST_COLS], U16, name="list%d" % t) for t in range(PACK)]
+        put_list = sb.tile([P, LIST_COLS], U16, name="put_list")
+        w_codes = sb.tile([P, 2 * N], U8, name="w_codes", align_bytes=64)
+        w_plane = sb.tile([P, N], U8, name="w_plane", align_bytes=64)
+        weights = sb.tile([P, N // P], F32, name="weights")
+        z = sb.tile([P, PACK * J], BF16, name="z", align_bytes=64)
+        pages = [sb.tile([P, E], F32, name="page%d" % b) for b in range(N // P)]
+
+        nc.vector.memset(w_plane[:].bitcast(U32), 0)
+        for page in pages:
+            nc.vector.memset(page[:], 0.0)
+
+        for t in (0, 1):
+            nc.sync.dma_start(lists[t][:], (offs, offs2)[t])
+            nc.sync.dma_start(steps[t][:], (ga, gb)[t])
+        for t, src in enumerate((ca, cb, cc, cd)):
+            nc.scalar.dma_start(tables[t][:], src)
+        for t in (2, 3):
+            nc.sync.dma_start(lists[t][:], (offs3, offs4)[t - 2])
+            nc.sync.dma_start(steps[t][:], (gc, gd)[t - 2])
+        nc.sync.dma_start(w_codes[:].bitcast(I32), w_words[0].bitcast(I32))
+        nc.sync.dma_start(put_list[:], offs5)
+        for quad in range(4):
+            nc.gpsimd.dma_start(
+                w_plane[32 * quad : 32 * quad + 4, :].bitcast(I32),
+                w_scales[0, 4 * quad : 4 * quad + 4, :].bitcast(I32),
+            )
+        with nc.allow_non_contiguous_dma(reason="one output weight a partition"):
+            nc.gpsimd.dma_start(weights[:], so.rearrange("(b p) o -> p (b o)", p=P))
+
+        def fetch(t, j0, j1):
+            nc.scalar.activation(
+                out=z[:, PACK * j0 + t : PACK * j1 : PACK],
+                in_=tables[t][:].indirect(lists[t][:, j0 // 16 : j1 // 16]),
+                func=COPY,
+                scale=steps[t][:],
+            )
+
+        def multiply(h):
+            codes = sb.tile([P, HALF], U32, name="codes%d" % h, align_bytes=64)
+            plane = sb.tile([P, HALF], U8, name="plane%d" % h, align_bytes=64)
+            nc.vector.quantize_mx(
+                out=codes[:].bitcast(FP8X4),
+                scales=plane[:],
+                in_=z[:, PACK * HALF * h : PACK * HALF * (h + 1)],
+            )
+            rows = []
+            for b in range(N // P):
+                acc = psum.tile([P, HALF], F32, name="acc%d%d" % (h, b))
+                nc.tensor.matmul_mx(
+                    out=acc[:],
+                    lhsT=w_codes[:, 2 * P * b : 2 * P * (b + 1)].bitcast(FP4X4),
+                    lhsT_scale=w_plane[:, P * b : P * (b + 1)],
+                    rhs=codes[:].bitcast(FP8X4),
+                    rhs_scale=plane[:],
+                    start=True,
+                    stop=True,
+                )
+                prod = sb.tile([P, HALF], F32, name="prod%d%d" % (h, b))
+                nc.vector.tensor_copy(out=prod[:], in_=acc[:])
+                rows.append(prod)
+            return rows
+
+        def put(h, b, prod):
+            nc.scalar.activation(
+                out=pages[b][:].indirect(put_list[:, h * HALF // 16 : (h + 1) * HALF // 16]),
+                in_=prod[:],
+                func=COPY,
+                scale=weights[:, b : b + 1],
+            )
+
+        fetch(0, 0, J)
+        fetch(1, 0, J)
+        prods = []
+        for h in range(2):
+            fetch(2, h * HALF, (h + 1) * HALF)
+            fetch(3, h * HALF, (h + 1) * HALF)
+            prods.append(multiply(h))
+        for h in range(2):
+            for b in range(N // P):
+                put(h, b, prods[h][b])
+        for b in range(N // P):
+            nc.sync.dma_start(out[P * b : P * (b + 1), :], pages[b][:])

@@ -38,26 +38,34 @@ def tile_list_fourtables_kernel(tc, ca, ga, cb, gb, cc, gc, cd, gd, w_words, w_s
         pages = [sb.tile([P, E], F32, name="page%d" % b) for b in range(N // P)]
 
         nc.vector.memset(w_plane[:].bitcast(U32), 0)
+        warm = sb.tile([P, 2], F32, name="warm")
+        nc.vector.memset(warm[:, 0:1], 0.0)
         for page in pages:
             nc.vector.memset(page[:], 0.0)
 
-        for t in (0, 1):
-            nc.sync.dma_start(lists[t][:], (offs, offs2)[t])
-            nc.sync.dma_start(steps[t][:], (ga, gb)[t])
-        for t, src in enumerate((ca, cb, cc, cd)):
-            nc.scalar.dma_start(tables[t][:], src)
-        for t in (2, 3):
-            nc.sync.dma_start(lists[t][:], (offs3, offs4)[t - 2])
-            nc.sync.dma_start(steps[t][:], (gc, gd)[t - 2])
+        nc.scalar.dma_start(steps[1][:], gb)
+        nc.scalar.dma_start(steps[3][:], gd)
+        nc.gpsimd.dma_start(steps[0][:], ga)
+        nc.gpsimd.dma_start(steps[2][:], gc)
+        with nc.allow_non_contiguous_dma(reason="one output weight a partition"):
+            nc.gpsimd.dma_start(weights[:], so.rearrange("(b p) o -> p (b o)", p=P))
+        nc.sync.dma_start(tables[1][:], cb)
+        nc.sync.dma_start(lists[1][:], offs2)
+        nc.sync.dma_start(lists[3][:], offs4)
+        nc.sync.dma_start(lists[0][:], offs)
+        nc.sync.dma_start(tables[3][:], cd)
+        nc.sync.dma_start(tables[0][:], ca)
+        nc.sync.dma_start(lists[2][:], offs3)
+        nc.sync.dma_start(tables[2][:], cc)
         nc.sync.dma_start(w_codes[:].bitcast(I32), w_words[0].bitcast(I32))
-        nc.sync.dma_start(put_list[:], offs5)
         for quad in range(4):
-            nc.gpsimd.dma_start(
+            nc.sync.dma_start(
                 w_plane[32 * quad : 32 * quad + 4, :].bitcast(I32),
                 w_scales[0, 4 * quad : 4 * quad + 4, :].bitcast(I32),
             )
-        with nc.allow_non_contiguous_dma(reason="one output weight a partition"):
-            nc.gpsimd.dma_start(weights[:], so.rearrange("(b p) o -> p (b o)", p=P))
+        nc.sync.dma_start(put_list[:], offs5)
+
+        nc.scalar.activation(out=warm[:, 1:2], in_=warm[:, 0:1], func=COPY)
 
         def fetch(t, j0, j1):
             nc.scalar.activation(
@@ -100,12 +108,12 @@ def tile_list_fourtables_kernel(tc, ca, ga, cb, gb, cc, gc, cd, gd, w_words, w_s
                 scale=weights[:, b : b + 1],
             )
 
-        fetch(0, 0, J)
         fetch(1, 0, J)
+        fetch(3, 0, J)
         prods = []
         for h in range(2):
+            fetch(0, h * HALF, (h + 1) * HALF)
             fetch(2, h * HALF, (h + 1) * HALF)
-            fetch(3, h * HALF, (h + 1) * HALF)
             prods.append(multiply(h))
         for h in range(2):
             for b in range(N // P):

@@ -17,6 +17,7 @@ COPY = mybir.ActivationFunctionType.Copy
 
 P = 128
 PACK = 4
+QUAD = 32
 HALF = J // 2
 LIST_COLS = J // 16
 
@@ -28,7 +29,8 @@ def tile_list_fourtables_kernel(tc, ca, ga, cb, gb, cc, gc, cd, gd, w_words, w_s
         psum = ctx.enter_context(tc.psum_pool(name="psum", bufs=1))
 
         tables = [sb.tile(list(src.shape), F32, name="table%d" % t) for t, src in enumerate((ca, cb, cc, cd))]
-        steps = [sb.tile([P, 1], F32, name="step%d" % t) for t in range(PACK)]
+        steps = [sb.tile([P, QUAD], F32, name="step%d" % t, align_bytes=64) for t in range(PACK)]
+        step_rows = {t: sb.tile([P, QUAD], F32, name="step_rows%d" % t, align_bytes=64) for t in (1, 3)}
         lists = [sb.tile([P, LIST_COLS], U16, name="list%d" % t) for t in range(PACK)]
         put_list = sb.tile([P, LIST_COLS], U16, name="put_list")
         w_codes = sb.tile([P, 2 * N], U8, name="w_codes", align_bytes=64)
@@ -37,33 +39,36 @@ def tile_list_fourtables_kernel(tc, ca, ga, cb, gb, cc, gc, cd, gd, w_words, w_s
         z = sb.tile([P, PACK * J], BF16, name="z", align_bytes=64)
         pages = [sb.tile([P, E], F32, name="page%d" % b) for b in range(N // P)]
 
+        for t in (1, 3):
+            nc.vector.memset(step_rows[t][:], 0.0)
         nc.vector.memset(w_plane[:].bitcast(U32), 0)
         warm = sb.tile([P, 2], F32, name="warm")
         nc.vector.memset(warm[:, 0:1], 0.0)
         for page in pages:
             nc.vector.memset(page[:], 0.0)
 
-        nc.scalar.dma_start(steps[1][:], gb)
-        nc.scalar.dma_start(steps[3][:], gd)
-        nc.gpsimd.dma_start(steps[0][:], ga)
-        nc.gpsimd.dma_start(steps[2][:], gc)
-        with nc.allow_non_contiguous_dma(reason="one output weight a partition"):
-            nc.gpsimd.dma_start(weights[:], so.rearrange("(b p) o -> p (b o)", p=P))
+        nc.gpsimd.dma_start(steps[0][:, 0:1], ga)
+        for t, src in ((1, gb), (3, gd)):
+            nc.scalar.dma_start(step_rows[t][0:P:QUAD, :], src.rearrange("(a i) o -> a (i o)", i=QUAD))
+            nc.vector.transpose(steps[t][:], step_rows[t][:])
         nc.sync.dma_start(tables[1][:], cb)
         nc.sync.dma_start(lists[1][:], offs2)
         nc.sync.dma_start(lists[3][:], offs4)
         nc.sync.dma_start(lists[0][:], offs)
         nc.sync.dma_start(tables[3][:], cd)
         nc.sync.dma_start(tables[0][:], ca)
-        nc.sync.dma_start(lists[2][:], offs3)
         nc.sync.dma_start(tables[2][:], cc)
+        nc.sync.dma_start(lists[2][:], offs3)
+        nc.sync.dma_start(steps[2][:, 0:1], gc)
         nc.sync.dma_start(w_codes[:].bitcast(I32), w_words[0].bitcast(I32))
         for quad in range(4):
-            nc.sync.dma_start(
+            (nc.sync if quad < 3 else nc.gpsimd).dma_start(
                 w_plane[32 * quad : 32 * quad + 4, :].bitcast(I32),
                 w_scales[0, 4 * quad : 4 * quad + 4, :].bitcast(I32),
             )
         nc.sync.dma_start(put_list[:], offs5)
+        with nc.allow_non_contiguous_dma(reason="one output weight a partition"):
+            nc.gpsimd.dma_start(weights[:], so.rearrange("(b p) o -> p (b o)", p=P))
 
         nc.scalar.activation(out=warm[:, 1:2], in_=warm[:, 0:1], func=COPY)
 
@@ -72,51 +77,50 @@ def tile_list_fourtables_kernel(tc, ca, ga, cb, gb, cc, gc, cd, gd, w_words, w_s
                 out=z[:, PACK * j0 + t : PACK * j1 : PACK],
                 in_=tables[t][:].indirect(lists[t][:, j0 // 16 : j1 // 16]),
                 func=COPY,
-                scale=steps[t][:],
+                scale=steps[t][:, 0:1],
             )
 
-        def multiply(h):
-            codes = sb.tile([P, HALF], U32, name="codes%d" % h, align_bytes=64)
-            plane = sb.tile([P, HALF], U8, name="plane%d" % h, align_bytes=64)
+        codes = sb.tile([P, J], U32, name="codes", align_bytes=64)
+        plane = sb.tile([P, J], U8, name="plane", align_bytes=64)
+
+        def quantize(j0, j1):
             nc.vector.quantize_mx(
-                out=codes[:].bitcast(FP8X4),
-                scales=plane[:],
-                in_=z[:, PACK * HALF * h : PACK * HALF * (h + 1)],
+                out=codes[:, j0:j1].bitcast(FP8X4),
+                scales=plane[:, j0:j1],
+                in_=z[:, PACK * j0 : PACK * j1],
             )
-            rows = []
-            for b in range(N // P):
-                acc = psum.tile([P, HALF], F32, name="acc%d%d" % (h, b))
-                nc.tensor.matmul_mx(
-                    out=acc[:],
-                    lhsT=w_codes[:, 2 * P * b : 2 * P * (b + 1)].bitcast(FP4X4),
-                    lhsT_scale=w_plane[:, P * b : P * (b + 1)],
-                    rhs=codes[:].bitcast(FP8X4),
-                    rhs_scale=plane[:],
-                    start=True,
-                    stop=True,
-                )
-                prod = sb.tile([P, HALF], F32, name="prod%d%d" % (h, b))
-                nc.vector.tensor_copy(out=prod[:], in_=acc[:])
-                rows.append(prod)
-            return rows
 
-        def put(h, b, prod):
+        def multiply(b, j0, j1):
+            acc = psum.tile([P, j1 - j0], F32, name="acc%d_%d" % (b, j0))
+            nc.tensor.matmul_mx(
+                out=acc[:],
+                lhsT=w_codes[:, 2 * P * b : 2 * P * (b + 1)].bitcast(FP4X4),
+                lhsT_scale=w_plane[:, P * b : P * (b + 1)],
+                rhs=codes[:, j0:j1].bitcast(FP8X4),
+                rhs_scale=plane[:, j0:j1],
+                start=True,
+                stop=True,
+            )
+            prod = sb.tile([P, j1 - j0], F32, name="prod%d_%d" % (b, j0))
+            nc.vector.tensor_copy(out=prod[:], in_=acc[:])
+            return prod
+
+        def put(b, j0, j1, prod):
             nc.scalar.activation(
-                out=pages[b][:].indirect(put_list[:, h * HALF // 16 : (h + 1) * HALF // 16]),
+                out=pages[b][:].indirect(put_list[:, j0 // 16 : j1 // 16]),
                 in_=prod[:],
                 func=COPY,
                 scale=weights[:, b : b + 1],
             )
 
-        fetch(1, 0, J)
-        fetch(3, 0, J)
-        prods = []
-        for h in range(2):
-            fetch(0, h * HALF, (h + 1) * HALF)
-            fetch(2, h * HALF, (h + 1) * HALF)
-            prods.append(multiply(h))
-        for h in range(2):
-            for b in range(N // P):
-                put(h, b, prods[h][b])
-        for b in range(N // P):
+        for t in (1, 3, 0):
+            fetch(t, 0, J)
+        for j0 in (0, HALF):
+            fetch(2, j0, j0 + HALF)
+            quantize(j0, j0 + HALF)
+        pieces = ((0, 0, HALF), (1, 0, J), (0, HALF, J))
+        prods = [multiply(*piece) for piece in pieces]
+        for piece, prod in zip(pieces, prods):
+            put(*piece, prod)
+        for b in (1, 0):
             nc.sync.dma_start(out[P * b : P * (b + 1), :], pages[b][:])

from contextlib import ExitStack

import concourse.mybir as mybir

K, J, N, E = 512, 256, 256, 512
FLOPS = 2 * K * N * J

F32 = mybir.dt.float32
BF16 = mybir.dt.bfloat16
I32 = mybir.dt.int32
U32 = mybir.dt.uint32
U16 = mybir.dt.uint16
U8 = mybir.dt.uint8
FP8X4 = mybir.dt.float8_e4m3fn_x4
FP4X4 = mybir.dt.float4_e2m1fn_x4
COPY = mybir.ActivationFunctionType.Copy

P = 128
PACK = 4
QUAD = 32
HALF = J // 2
LIST_COLS = J // 16


def tile_list_fourtables_kernel(tc, ca, ga, cb, gb, cc, gc, cd, gd, w_words, w_scales, so, offs, offs2, offs3, offs4, offs5, out):
    nc = tc.nc
    with ExitStack() as ctx:
        sb = ctx.enter_context(tc.tile_pool(name="sb", bufs=1))
        psum = ctx.enter_context(tc.psum_pool(name="psum", bufs=1))

        tables = [sb.tile(list(src.shape), F32, name="table%d" % t) for t, src in enumerate((ca, cb, cc, cd))]
        steps = [sb.tile([P, QUAD], F32, name="step%d" % t, align_bytes=64) for t in range(PACK)]
        step_rows = {t: sb.tile([P, QUAD], F32, name="step_rows%d" % t, align_bytes=64) for t in (1, 3)}
        lists = [sb.tile([P, LIST_COLS], U16, name="list%d" % t) for t in range(PACK)]
        put_list = sb.tile([P, LIST_COLS], U16, name="put_list")
        w_codes = sb.tile([P, 2 * N], U8, name="w_codes", align_bytes=64)
        w_plane = sb.tile([P, N], U8, name="w_plane", align_bytes=64)
        weights = sb.tile([P, N // P], F32, name="weights")
        z = sb.tile([P, PACK * J], BF16, name="z", align_bytes=64)
        pages = [sb.tile([P, E], F32, name="page%d" % b) for b in range(N // P)]

        for t in (1, 3):
            nc.vector.memset(step_rows[t][:], 0.0)
        nc.vector.memset(w_plane[:].bitcast(U32), 0)
        warm = sb.tile([P, 2], F32, name="warm")
        nc.vector.memset(warm[:, 0:1], 0.0)
        for page in pages:
            nc.vector.memset(page[:], 0.0)

        nc.gpsimd.dma_start(steps[0][:, 0:1], ga)
        for t, src in ((1, gb), (3, gd)):
            nc.scalar.dma_start(step_rows[t][0:P:QUAD, :], src.rearrange("(a i) o -> a (i o)", i=QUAD))
            nc.vector.transpose(steps[t][:], step_rows[t][:])
        nc.sync.dma_start(tables[1][:], cb)
        nc.sync.dma_start(lists[1][:], offs2)
        nc.sync.dma_start(lists[3][:], offs4)
        nc.sync.dma_start(lists[0][:], offs)
        nc.sync.dma_start(tables[3][:], cd)
        nc.sync.dma_start(tables[0][:], ca)
        nc.sync.dma_start(tables[2][:], cc)
        nc.sync.dma_start(lists[2][:], offs3)
        nc.sync.dma_start(steps[2][:, 0:1], gc)
        nc.sync.dma_start(w_codes[:].bitcast(I32), w_words[0].bitcast(I32))
        for quad in range(4):
            (nc.sync if quad < 3 else nc.gpsimd).dma_start(
                w_plane[32 * quad : 32 * quad + 4, :].bitcast(I32),
                w_scales[0, 4 * quad : 4 * quad + 4, :].bitcast(I32),
            )
        nc.sync.dma_start(put_list[:], offs5)
        with nc.allow_non_contiguous_dma(reason="one output weight a partition"):
            nc.gpsimd.dma_start(weights[:], so.rearrange("(b p) o -> p (b o)", p=P))

        nc.scalar.activation(out=warm[:, 1:2], in_=warm[:, 0:1], func=COPY)

        def fetch(t, j0, j1):
            nc.scalar.activation(
                out=z[:, PACK * j0 + t : PACK * j1 : PACK],
                in_=tables[t][:].indirect(lists[t][:, j0 // 16 : j1 // 16]),
                func=COPY,
                scale=steps[t][:, 0:1],
            )

        codes = sb.tile([P, J], U32, name="codes", align_bytes=64)
        plane = sb.tile([P, J], U8, name="plane", align_bytes=64)

        def quantize(j0, j1):
            nc.vector.quantize_mx(
                out=codes[:, j0:j1].bitcast(FP8X4),
                scales=plane[:, j0:j1],
                in_=z[:, PACK * j0 : PACK * j1],
            )

        def multiply(b, j0, j1):
            acc = psum.tile([P, j1 - j0], F32, name="acc%d_%d" % (b, j0))
            nc.tensor.matmul_mx(
                out=acc[:],
                lhsT=w_codes[:, 2 * P * b : 2 * P * (b + 1)].bitcast(FP4X4),
                lhsT_scale=w_plane[:, P * b : P * (b + 1)],
                rhs=codes[:, j0:j1].bitcast(FP8X4),
                rhs_scale=plane[:, j0:j1],
                start=True,
                stop=True,
            )
            prod = sb.tile([P, j1 - j0], F32, name="prod%d_%d" % (b, j0))
            nc.vector.tensor_copy(out=prod[:], in_=acc[:])
            return prod

        def put(b, j0, j1, prod):
            nc.scalar.activation(
                out=pages[b][:].indirect(put_list[:, j0 // 16 : j1 // 16]),
                in_=prod[:],
                func=COPY,
                scale=weights[:, b : b + 1],
            )

        for t in (1, 3, 0):
            fetch(t, 0, J)
        for j0 in (0, HALF):
            fetch(2, j0, j0 + HALF)
            quantize(j0, j0 + HALF)
        pieces = ((0, 0, HALF), (1, 0, J), (0, HALF, J))
        prods = [multiply(*piece) for piece in pieces]
        for piece, prod in zip(pieces, prods):
            put(*piece, prod)
        for b in (1, 0):
            nc.sync.dma_start(out[P * b : P * (b + 1), :], pages[b][:])
